import numpy as np
import ml_dtypes


def mxq(x, axis, fmt="e4m3"):
    dtype, down = {"e4m3": (ml_dtypes.float8_e4m3fn, 7), "e5m2": (ml_dtypes.float8_e5m2, 14)}[fmt]
    v = np.moveaxis(np.asarray(x, np.float32).astype(ml_dtypes.bfloat16).astype(np.float64), axis, -1)
    blocks = v.reshape(v.shape[:-1] + (-1, 32))
    amax = np.abs(blocks).max(-1, keepdims=True)
    byte = np.maximum(np.where(amax > 0, np.frexp(amax)[1] - 1 + 127, 0) - down, 1)
    scale = np.exp2(byte - 127.0)
    codes = (blocks / scale).astype(np.float32).astype(dtype).astype(np.float64)
    return np.moveaxis((codes * scale).reshape(v.shape), -1, axis)


WIDE = False


def mx_kscale(k):
    if not WIDE:
        return np.ones(k)
    levels = np.array([10, -10, 5, -5, 0])
    if k % 512:
        return np.exp2(np.random.permutation(np.resize(levels, k // 32))).repeat(32)
    a = np.empty((k // 512, 16))
    for p in range(k // 512):
        a[p, :8] = np.random.permutation(np.resize(levels, 8))
        for g in range(8):
            far = levels[np.abs(levels - a[p, g]) >= 10]
            a[p, g + 8] = far[np.random.randint(len(far))]
    return np.exp2(a.ravel()).repeat(32)


def f64(x):
    return np.asarray(x).astype(np.float64)


def striped(idx):
    return np.tile(idx.reshape(-1, 16).T, (8, 1)).astype(np.uint16)


def unstriped(offs):
    return offs[:16].T.reshape(-1).astype(np.int64)


def striped8(idx):
    return np.concatenate([x.reshape(-1, 16).T for x in idx]).astype(np.uint16)


def runs(offs, k):
    lists = np.stack([offs[16 * r : 16 * r + 16].T.reshape(-1) for r in range(8)]).astype(np.int64)
    return lists[np.arange(k) % 512 // 64]


def pack_weight(w):
    k, n = w.shape
    w = f64(np.asarray(w, np.float32).astype(ml_dtypes.bfloat16)).reshape(k // 32, 32, n)
    amax = np.abs(w).max(1)
    byte = np.clip(np.where(amax > 0, np.frexp(amax)[1] - 1 + 127 - 7, 1), 1, 254)
    scaled = (w * np.exp2(127.0 - byte)[:, None, :]).reshape(k, n).astype(np.float32)
    words = np.ascontiguousarray(scaled.reshape(k // 512, 128, 4, n).transpose(0, 1, 3, 2)).astype(ml_dtypes.float8_e4m3fn).view(np.uint8)
    return words, np.ascontiguousarray(byte.astype(np.uint8).reshape(k // 512, 16, n))


def unpack_weight(words, scales):
    g, p, n, _ = words.shape
    vals = np.ascontiguousarray(words).view(ml_dtypes.float8_e4m3fn).astype(np.float64) * np.repeat(np.exp2(scales.astype(np.float64) - 127.0), 8, axis=1)[..., None]
    return vals.transpose(0, 1, 3, 2).reshape(g * 512, n)

def planes(y):
    n, m = y.shape
    v = y.astype(np.float32).astype(ml_dtypes.bfloat16).astype(np.float64).reshape(n // 32, 32, m)
    top = np.abs(v).max(1)
    byte = np.clip(np.where(top > 0, np.frexp(top)[1] - 1 + 127 - 7, 1), 1, 254)
    codes = (v * np.exp2(127.0 - byte)[:, None, :]).reshape(n, m).astype(np.float32).astype(ml_dtypes.float8_e4m3fn).view(np.uint8)
    words = codes.reshape(n // 512, 128, 4, m).transpose(0, 1, 3, 2)
    return np.ascontiguousarray(words), np.ascontiguousarray(byte.astype(np.uint8).reshape(n // 512, 16, m))


K, T, S, G, H = 512, 2048, 512, 2048, 512


def setup_inputs():
    n = np.random.standard_normal
    s = mx_kscale(K)[:, None]
    packed_xT = pack_weight(n((K, T)) * s)
    packed_dT = pack_weight(n((K, G)) / s)
    return {
        "x_words": packed_xT[0],
        "x_scales": packed_xT[1],
        "d_words": packed_dT[0],
        "d_scales": packed_dT[1],
        "gs": (np.random.uniform(0.5, 1.5, (K, 1)) * s).astype(np.float32),
        "offs": striped(np.random.permutation(T)[:S]),
        "k1": striped8(np.random.randint(0, G, (8, H))),
        "n1": striped8(np.stack([np.random.permutation(S) for _ in range(8)])),
        "n2": striped8(np.stack([np.random.permutation(S) for _ in range(8)])),
        "k2": striped8(np.random.randint(0, G, (8, H))),
    }


def reference(x_words, x_scales, d_words, d_scales, gs, offs, k1, n1, n2, k2):
    d_k2 = unpack_weight(d_words, d_scales)[np.arange(K)[:, None], runs(k2, K)]
    d_k1 = unpack_weight(d_words, d_scales)[np.arange(K)[:, None], runs(k1, K)]
    xq = unpack_weight(x_words, x_scales)[:, unstriped(offs)]
    h = 0.0625 * (d_k1.T @ xq)
    z = f64(gs) * (h / (np.abs(h[np.arange(H)[:, None], runs(n1, H)]) + np.abs(h[np.arange(H)[:, None], runs(n2, H)]) + 0.5))
    out_0 = 0.0625 * ((d_k2.T @ mxq(z, 0, "e4m3")))
    return (out_0,) + planes(out_0)

@@ -1,0 +1,250 @@
+from contextlib import ExitStack
+
+import concourse.mybir as mybir
+
+F32 = mybir.dt.float32
+BF16 = mybir.dt.bfloat16
+I32 = mybir.dt.int32
+U32 = mybir.dt.uint32
+U16 = mybir.dt.uint16
+U8 = mybir.dt.uint8
+FP8X4 = mybir.dt.float8_e4m3fn_x4
+ACT = mybir.ActivationFunctionType
+ALU = mybir.AluOpType
+
+P = 128
+PACK = 4
+K = 512
+TABLE = 2048
+S = 512
+H = 512
+LIST_COLS = 32
+HALF = 256
+UNIT = 128
+
+FLOPS = 2 * 2 * K * H * S
+
+
+def tile_picked_pqdiv_none_po_kernel(
+    tc, x_words, x_scales, d_words, d_scales, gs, offs, k1, n1, n2, k2, out_0, out_1, out_2
+):
+    nc = tc.nc
+    with ExitStack() as ctx:
+        pool = ctx.enter_context(tc.tile_pool(name="held", bufs=1))
+        psum = ctx.enter_context(tc.psum_pool(name="psum", bufs=1))
+
+        def sb(name, shape, dtype, tag=None):
+            return pool.tile(shape, dtype, name=name, tag=tag or name, align_bytes=64)
+
+        lists = {name: sb("list_" + name, [P, LIST_COLS], U16) for name in ("offs", "k1", "n1", "n2", "k2")}
+        d_word_table = sb("d_word_table", [P, TABLE], I32)
+        x_word_table = sb("x_word_table", [P, TABLE], I32)
+        d_byte_table = sb("d_byte_table", [P, TABLE], U8)
+        x_byte_table = sb("x_byte_table", [P, TABLE], U8)
+        gain = sb("gain", [P, PACK], F32)
+        warm = sb("warm", [P, 2], F32)
+        out_bytes = sb("out_bytes", [P, S], U8)
+
+        nc.gpsimd.memset(d_byte_table[:].bitcast(I32), 0)
+        nc.vector.memset(x_byte_table[:].bitcast(I32), 0)
+        nc.gpsimd.memset(warm[:, 0:1], 1.0)
+        nc.scalar.activation(warm[:, 1:2], warm[:, 0:1], ACT.Abs_reciprocal_sqrt)
+
+        x_rows = x_scales[0].bitcast(I32)
+
+        def load_token_bytes(q):
+            nc.sync.dma_start(x_byte_table[32 * q : 32 * q + 4, :].bitcast(I32), x_rows[4 * q : 4 * q + 4, :])
+
+        nc.sync.dma_start(lists["k1"][:], k1)
+        nc.sync.dma_start(d_byte_table[0:P:8, :].bitcast(I32), d_scales[0].bitcast(I32))
+        nc.sync.dma_start(lists["k2"][:], k2)
+        nc.sync.dma_start(d_word_table[:], d_words[0].rearrange("p n t -> p (n t)").bitcast(I32))
+        nc.sync.dma_start(lists["offs"][:], offs)
+        load_token_bytes(0)
+        load_token_bytes(1)
+        nc.sync.dma_start(x_word_table[:], x_words[0].rearrange("p n t -> p (n t)").bitcast(I32))
+        load_token_bytes(2)
+        load_token_bytes(3)
+        nc.sync.dma_start(lists["n1"][:], n1)
+        nc.sync.dma_start(lists["n2"][:], n2)
+        nc.scalar.dma_start(gain[:], gs.rearrange("(p t) o -> p (t o)", t=PACK))
+
+        def coded_bytes(name):
+            picked = sb("picked_bytes_" + name, [P, H], U8)
+            nc.vector.tensor_copy(picked[:], d_byte_table[:].indirect(lists[name][:]))
+            dealt = sb("dealt_bytes_" + name, [P, H], U8)
+            nc.vector.tensor_copy(
+                dealt[:].rearrange("p (t c i) -> p c t i", t=PACK, i=16),
+                picked[:].rearrange("p (c i t) -> p c t i", t=PACK, i=16),
+            )
+            for a in range(1, 4):
+                nc.sync.dma_start(dealt[a:P:32, :].bitcast(I32), dealt[8 * a : P : 32, :].bitcast(I32))
+            return dealt
+
+        def pick_words(name, tag=None):
+            picked = sb("picked_words_" + name, [P, H], U32, tag)
+            nc.vector.tensor_copy(picked[:], d_word_table[:].bitcast(U32).indirect(lists[name][:]))
+            return picked
+
+        def deal_words(name, picked, tag=None):
+            dealt = sb("dealt_words_" + name, [P, H], U32, tag)
+            nc.vector.tensor_copy(
+                dealt[:].bitcast(I32).rearrange("p (t c i) -> p c t i", t=PACK, i=4),
+                picked[:].bitcast(I32).rearrange("p (c i t) -> p c t i", t=PACK, i=4),
+            )
+            return dealt
+
+        first_bytes = coded_bytes("k1")
+        second_bytes = coded_bytes("k2")
+        first_words = deal_words("k1", pick_words("k1"))
+        token_words = sb("token_words", [P, S], U32)
+        nc.vector.tensor_copy(token_words[:], x_word_table[:].bitcast(U32).indirect(lists["offs"][:]))
+        token_bytes = sb("token_bytes", [P, S], U8)
+        nc.vector.tensor_copy(token_bytes[:], x_byte_table[:].indirect(lists["offs"][:]))
+
+        hidden = []
+        sizes = []
+        for t in range(PACK):
+            cols = slice(P * t, P * (t + 1))
+            bank = psum.tile([P, S], F32, name="hidden%d" % t)
+            nc.tensor.matmul_mx(
+                bank[:],
+                lhsT=first_words[:, cols].bitcast(FP8X4),
+                lhsT_scale=first_bytes[:, cols],
+                rhs=token_words[:].bitcast(FP8X4),
+                rhs_scale=token_bytes[:],
+                start=True,
+                stop=True,
+            )
+            size = sb("size%d" % t, [P, S], F32)
+            nc.scalar.activation(size[:], bank[:], ACT.Abs, scale=0.0625)
+            hidden.append(bank)
+            sizes.append(size)
+
+        second_picked = pick_words("k2", "x_byte_table")
+
+        out_rows = out_0.rearrange("(p t) j -> p t j", t=PACK)
+        out_words_dram = out_1[0].rearrange("p n t -> p (n t)").bitcast(I32)
+        inverses = {}
+
+        def look_up(half, rows, first_tags):
+            entries = slice(HALF // 16 * half, HALF // 16 * (half + 1))
+            total = sb("total%d_%d" % (half, rows[0]), [P, 2, HALF], F32)
+            firsts = []
+            for t, tag in zip(rows, first_tags):
+                first = sb("first%d_%d" % (half, t), [P, HALF], F32, tag)
+                nc.vector.tensor_copy(first[:], sizes[t][:].indirect(lists["n1"][:, entries]))
+                firsts.append(first)
+            for u, t in enumerate(rows):
+                nc.vector.tensor_tensor(total[:, u, :], sizes[t][:].indirect(lists["n2"][:, entries]), firsts[u][:], ALU.add)
+            return total
+
+        def invert_pair(half, rows, total):
+            root = sb("root%d_%d" % (half, rows[0]), [P, 2, HALF], F32, "root")
+            inverse = sb("inverse%d_%d" % (half, rows[0]), [P, 2, HALF], F32)
+            nc.scalar.activation(root[:], total[:], ACT.Abs_reciprocal_sqrt, bias=0.5)
+            nc.scalar.activation(inverse[:], root[:], ACT.Square, scale=0.25)
+            for u, t in enumerate(rows):
+                inverses[half, t] = inverse[:, u, :]
+
+        def invert_apart(half, rows, total):
+            root = sb("root%d_%d" % (half, rows[0]), [P, 2, HALF], F32, "root")
+            inverse = sb("inverse%d_%d" % (half, rows[0]), [P, 2, HALF], F32)
+            for u in range(2):
+                nc.scalar.activation(root[:, u, :], total[:, u, :], ACT.Abs_reciprocal_sqrt, bias=0.5)
+            for u, t in enumerate(rows):
+                nc.scalar.activation(inverse[:, u, :], root[:, u, :], ACT.Square, scale=0.25)
+                inverses[half, t] = inverse[:, u, :]
+
+        def divide(half, tag=None):
+            z = sb("z%d" % half, [P, PACK, HALF], BF16, tag)
+            for t in range(PACK):
+                nc.vector.scalar_tensor_tensor(
+                    z[:, t, :],
+                    hidden[t][:, HALF * half : HALF * (half + 1)],
+                    gain[:, t : t + 1],
+                    inverses[half, t],
+                    ALU.mult,
+                    ALU.mult,
+                )
+            return z
+
+        def weave(copy, name, source, width):
+            woven = sb(name, [P, width, PACK], BF16)
+            copy(woven[:].rearrange("p (c i) t -> p c t i", i=4), source.rearrange("p t (c i) -> p c t i", i=4))
+            return woven
+
+        def quantise_z(name, woven, width):
+            z_words = sb("z_words" + name, [P, width], U32)
+            z_bytes = sb("z_bytes" + name, [P, width], U8)
+            nc.vector.quantize_mx(z_words[:].bitcast(FP8X4), z_bytes[:], woven[:].rearrange("p n t -> p (n t)"))
+            return z_words, z_bytes
+
+        def second_product(unit, second_words, z_words, z_bytes):
+            bank = psum.tile([P, PACK, UNIT], F32, name="product%d" % unit)
+            for t in range(PACK):
+                cols = slice(P * t, P * (t + 1))
+                nc.tensor.matmul_mx(
+                    bank[:, t, :],
+                    lhsT=second_words[:, cols].bitcast(FP8X4),
+                    lhsT_scale=second_bytes[:, cols],
+                    rhs=z_words.bitcast(FP8X4),
+                    rhs_scale=z_bytes,
+                    start=True,
+                    stop=True,
+                )
+            return bank
+
+        def hand_out(unit, bank):
+            result = sb("result%d" % unit, [P, PACK, UNIT], F32)
+            nc.scalar.activation(result[:], bank[:], ACT.Copy, scale=0.0625)
+            nc.sync.dma_start(out_rows[:, :, UNIT * unit : UNIT * (unit + 1)], result[:])
+            return result
+
+        def quantise_out(name, woven, cols, width):
+            words = sb("out_words" + name, [P, width], U32)
+            nc.vector.quantize_mx(words[:].bitcast(FP8X4), out_bytes[:, cols], woven[:].rearrange("p n t -> p (n t)"))
+            nc.sync.dma_start(out_words_dram[:, cols], words[:].bitcast(I32))
+
+        invert_pair(0, (0, 1), look_up(0, (0, 1), (None, None)))
+        invert_pair(0, (2, 3), look_up(0, (2, 3), (None, None)))
+        invert_pair(1, (0, 1), look_up(1, (0, 1), ("first0_2", "first0_3")))
+        z_low = divide(0)
+        total = look_up(1, (2, 3), ("inverse0_0", "inverse0_2"))
+        woven_low = weave(nc.scalar.copy, "z_woven0", z_low[:], HALF)
+        invert_apart(1, (2, 3), total)
+        second_words = deal_words("k2", second_picked, "z0")
+        z_words, z_bytes = quantise_z("0", woven_low, HALF)
+        banks = []
+        for unit in range(2):
+            cols = slice(UNIT * unit, UNIT * (unit + 1))
+            banks.append(second_product(unit, second_words, z_words[:, cols], z_bytes[:, cols]))
+        z_high = divide(1, "z_woven0")
+        woven_high = []
+        for n in range(2):
+            woven_high.append(
+                weave(nc.vector.tensor_copy, "z_woven1_%d" % n, z_high[:, :, UNIT * n : UNIT * (n + 1)], UNIT)
+            )
+        for n in range(2):
+            z_words, z_bytes = quantise_z("1_%d" % n, woven_high[n], UNIT)
+            banks.append(second_product(2 + n, second_words, z_words[:], z_bytes[:]))
+
+        out_woven_low = sb("out_woven0", [P, HALF, PACK], BF16)
+        for unit in range(2):
+            nc.scalar.activation(
+                out_woven_low[:, UNIT * unit : UNIT * (unit + 1), :],
+                banks[unit][:].rearrange("p t n -> p n t"),
+                ACT.Copy,
+                scale=0.0625,
+            )
+        quantise_out("0", out_woven_low, slice(0, HALF), HALF)
+        for unit in (2, 3):
+            result = hand_out(unit, banks[unit])
+            woven = weave(nc.vector.tensor_copy, "out_woven%d" % unit, result[:], UNIT)
+            quantise_out("%d" % unit, woven, slice(UNIT * unit, UNIT * (unit + 1)), UNIT)
+        for unit in (0, 1):
+            hand_out(unit, banks[unit])
+        out_scale_rows = out_2[0].bitcast(I32)
+        for q in range(4):
+            queue = nc.sync if q % 2 == 0 else nc.scalar
+            queue.dma_start(out_scale_rows[4 * q : 4 * q + 4, :], out_bytes[32 * q : 32 * q + 4, :].bitcast(I32))

@@ -21,6 +21,8 @@ H = 512
 LIST_COLS = 32
 HALF = 256
 UNIT = 128
+ROOTS = 4 * TABLE
+TOTALS = ROOTS + 4096
 
 FLOPS = 2 * 2 * K * H * S
 
@@ -31,76 +33,96 @@ def tile_picked_pqdiv_none_po_kernel(
     nc = tc.nc
     with ExitStack() as ctx:
         pool = ctx.enter_context(tc.tile_pool(name="held", bufs=1))
+        reused = ctx.enter_context(tc.tile_pool(name="reused", bufs=1))
         psum = ctx.enter_context(tc.psum_pool(name="psum", bufs=1))
 
         def sb(name, shape, dtype, tag=None):
             return pool.tile(shape, dtype, name=name, tag=tag or name, align_bytes=64)
 
+        def at(offset, name, shape, dtype):
+            return reused.tile(shape, dtype, name=name, align_bytes=64, offset=offset)
+
         lists = {name: sb("list_" + name, [P, LIST_COLS], U16) for name in ("offs", "k1", "n1", "n2", "k2")}
         d_word_table = sb("d_word_table", [P, TABLE], I32)
-        x_word_table = sb("x_word_table", [P, TABLE], I32)
+        x_word_table = at(0, "x_word_table", [P, TABLE], I32)
         d_byte_table = sb("d_byte_table", [P, TABLE], U8)
         x_byte_table = sb("x_byte_table", [P, TABLE], U8)
         gain = sb("gain", [P, PACK], F32)
         warm = sb("warm", [P, 2], F32)
         out_bytes = sb("out_bytes", [P, S], U8)
 
-        nc.gpsimd.memset(d_byte_table[:].bitcast(I32), 0)
+        token_bytes = sb("token_bytes", [P, S], U8)
+
+        sixteenths = [sb("sixteenth%d" % t, [P, 1], F32) for t in range(PACK)]
+        zero = at(ROOTS + 2048, "zero", [P, 1], F32)
+
         nc.vector.memset(x_byte_table[:].bitcast(I32), 0)
+        nc.gpsimd.memset(d_byte_table[:].bitcast(I32), 0)
         nc.gpsimd.memset(warm[:, 0:1], 1.0)
+        nc.gpsimd.memset(token_bytes[:].bitcast(I32), 0)
+        nc.gpsimd.memset(zero[:], 0.0)
+        for sixteenth in sixteenths:
+            nc.gpsimd.memset(sixteenth[:], 0.0625)
         nc.scalar.activation(warm[:, 1:2], warm[:, 0:1], ACT.Abs_reciprocal_sqrt)
 
-        x_rows = x_scales[0].bitcast(I32)
-
-        def load_token_bytes(q):
-            nc.sync.dma_start(x_byte_table[32 * q : 32 * q + 4, :].bitcast(I32), x_rows[4 * q : 4 * q + 4, :])
-
         nc.sync.dma_start(lists["k1"][:], k1)
-        nc.sync.dma_start(d_byte_table[0:P:8, :].bitcast(I32), d_scales[0].bitcast(I32))
         nc.sync.dma_start(lists["k2"][:], k2)
-        nc.sync.dma_start(d_word_table[:], d_words[0].rearrange("p n t -> p (n t)").bitcast(I32))
+        nc.sync.dma_start(d_byte_table[0:P:8, :].bitcast(I32), d_scales[0].bitcast(I32))
         nc.sync.dma_start(lists["offs"][:], offs)
-        load_token_bytes(0)
-        load_token_bytes(1)
-        nc.sync.dma_start(x_word_table[:], x_words[0].rearrange("p n t -> p (n t)").bitcast(I32))
-        load_token_bytes(2)
-        load_token_bytes(3)
+        nc.sync.dma_start(x_byte_table[0:P:8, :].bitcast(I32), x_scales[0].bitcast(I32))
+        nc.sync.dma_start(d_word_table[:], d_words[0].rearrange("p n t -> p (n t)").bitcast(I32))
         nc.sync.dma_start(lists["n1"][:], n1)
         nc.sync.dma_start(lists["n2"][:], n2)
-        nc.scalar.dma_start(gain[:], gs.rearrange("(p t) o -> p (t o)", t=PACK))
+        nc.sync.dma_start(gain[:], gs.rearrange("(p t) o -> p (t o)", t=PACK))
+        nc.sync.dma_start(x_word_table[:], x_words[0].rearrange("p n t -> p (n t)").bitcast(I32))
 
-        def coded_bytes(name):
-            picked = sb("picked_bytes_" + name, [P, H], U8)
-            nc.vector.tensor_copy(picked[:], d_byte_table[:].indirect(lists[name][:]))
-            dealt = sb("dealt_bytes_" + name, [P, H], U8)
+        def pick(name, table, dtype, index):
+            picked = sb(name, [P, H], dtype)
+            nc.vector.tensor_copy(picked[:], table.indirect(lists[index][:]))
+            return picked
+
+        def deal_bytes(dealt, picked):
             nc.vector.tensor_copy(
                 dealt[:].rearrange("p (t c i) -> p c t i", t=PACK, i=16),
                 picked[:].rearrange("p (c i t) -> p c t i", t=PACK, i=16),
             )
             for a in range(1, 4):
                 nc.sync.dma_start(dealt[a:P:32, :].bitcast(I32), dealt[8 * a : P : 32, :].bitcast(I32))
-            return dealt
 
-        def pick_words(name, tag=None):
-            picked = sb("picked_words_" + name, [P, H], U32, tag)
-            nc.vector.tensor_copy(picked[:], d_word_table[:].bitcast(U32).indirect(lists[name][:]))
-            return picked
-
-        def deal_words(name, picked, tag=None):
-            dealt = sb("dealt_words_" + name, [P, H], U32, tag)
+        def deal_words(dealt, picked):
             nc.vector.tensor_copy(
                 dealt[:].bitcast(I32).rearrange("p (t c i) -> p c t i", t=PACK, i=4),
                 picked[:].bitcast(I32).rearrange("p (c i t) -> p c t i", t=PACK, i=4),
             )
-            return dealt
 
-        first_bytes = coded_bytes("k1")
-        second_bytes = coded_bytes("k2")
-        first_words = deal_words("k1", pick_words("k1"))
-        token_words = sb("token_words", [P, S], U32)
-        nc.vector.tensor_copy(token_words[:], x_word_table[:].bitcast(U32).indirect(lists["offs"][:]))
-        token_bytes = sb("token_bytes", [P, S], U8)
-        nc.vector.tensor_copy(token_bytes[:], x_byte_table[:].indirect(lists["offs"][:]))
+        first_picked_bytes = pick("first_picked_bytes", d_byte_table[:], U8, "k1")
+        second_picked_bytes = pick("second_picked_bytes", d_byte_table[:], U8, "k2")
+        first_bytes = sb("first_bytes", [P, H], U8)
+        deal_bytes(first_bytes, first_picked_bytes)
+        token_picked_bytes = pick("token_picked_bytes", x_byte_table[:], U8, "offs")
+        for a in range(4):
+            nc.sync.dma_start(token_bytes[a:P:32, :].bitcast(I32), token_picked_bytes[8 * a : P : 32, :].bitcast(I32))
+        first_picked_words = sb("first_picked_words", [P, H], U32)
+        first_words = sb("first_words", [P, H], U32)
+        for half in range(2):
+            nc.vector.tensor_copy(
+                first_picked_words[:, HALF * half : HALF * (half + 1)],
+                d_word_table[:].bitcast(U32).indirect(lists["k1"][:, 16 * half : 16 * (half + 1)]),
+            )
+        for half in range(2):
+            nc.vector.tensor_copy(
+                first_words[:].bitcast(I32).rearrange("p (t c i) -> p c t i", t=PACK, i=4)[:, 16 * half : 16 * (half + 1)],
+                first_picked_words[:, HALF * half : HALF * (half + 1)]
+                .bitcast(I32)
+                .rearrange("p (c i t) -> p c t i", t=PACK, i=4),
+            )
+        token_words = pick("token_words", x_word_table[:].bitcast(U32), U32, "offs")
+        second_picked_words = at(0, "second_picked_words", [P, H], U32)
+        nc.vector.tensor_copy(second_picked_words[:], d_word_table[:].bitcast(U32).indirect(lists["k2"][:]))
+        second_bytes = at(4 * H, "second_bytes", [P, H], U8)
+        deal_bytes(second_bytes, second_picked_bytes)
+        second_words = sb("second_words", [P, H], U32)
+        deal_words(second_words, second_picked_words)
 
         hidden = []
         sizes = []
@@ -117,70 +139,43 @@ def tile_picked_pqdiv_none_po_kernel(
                 stop=True,
             )
             size = sb("size%d" % t, [P, S], F32)
-            nc.scalar.activation(size[:], bank[:], ACT.Abs, scale=0.0625)
+            nc.scalar.activation(size[:], bank[:], ACT.Abs, bias=zero[:], scale=sixteenths[t][:])
             hidden.append(bank)
             sizes.append(size)
 
-        second_picked = pick_words("k2", "x_byte_table")
-
         out_rows = out_0.rearrange("(p t) j -> p t j", t=PACK)
         out_words_dram = out_1[0].rearrange("p n t -> p (n t)").bitcast(I32)
-        inverses = {}
 
-        def look_up(half, rows, first_tags):
-            entries = slice(HALF // 16 * half, HALF // 16 * (half + 1))
-            total = sb("total%d_%d" % (half, rows[0]), [P, 2, HALF], F32)
-            firsts = []
-            for t, tag in zip(rows, first_tags):
-                first = sb("first%d_%d" % (half, t), [P, HALF], F32, tag)
+        def look_up(name, rows, start, firsts, total, root):
+            width = total.shape[-1]
+            entries = slice(start // 16, (start + width) // 16)
+            for t, first in zip(rows, firsts):
                 nc.vector.tensor_copy(first[:], sizes[t][:].indirect(lists["n1"][:, entries]))
-                firsts.append(first)
             for u, t in enumerate(rows):
                 nc.vector.tensor_tensor(total[:, u, :], sizes[t][:].indirect(lists["n2"][:, entries]), firsts[u][:], ALU.add)
-            return total
-
-        def invert_pair(half, rows, total):
-            root = sb("root%d_%d" % (half, rows[0]), [P, 2, HALF], F32, "root")
-            inverse = sb("inverse%d_%d" % (half, rows[0]), [P, 2, HALF], F32)
+            inverse = sb("inverse" + name, [P, 2, width], F32)
             nc.scalar.activation(root[:], total[:], ACT.Abs_reciprocal_sqrt, bias=0.5)
             nc.scalar.activation(inverse[:], root[:], ACT.Square, scale=0.25)
-            for u, t in enumerate(rows):
-                inverses[half, t] = inverse[:, u, :]
+            return inverse
 
-        def invert_apart(half, rows, total):
-            root = sb("root%d_%d" % (half, rows[0]), [P, 2, HALF], F32, "root")
-            inverse = sb("inverse%d_%d" % (half, rows[0]), [P, 2, HALF], F32)
-            for u in range(2):
-                nc.scalar.activation(root[:, u, :], total[:, u, :], ACT.Abs_reciprocal_sqrt, bias=0.5)
-            for u, t in enumerate(rows):
-                nc.scalar.activation(inverse[:, u, :], root[:, u, :], ACT.Square, scale=0.25)
-                inverses[half, t] = inverse[:, u, :]
-
-        def divide(half, tag=None):
-            z = sb("z%d" % half, [P, PACK, HALF], BF16, tag)
-            for t in range(PACK):
-                nc.vector.scalar_tensor_tensor(
-                    z[:, t, :],
-                    hidden[t][:, HALF * half : HALF * (half + 1)],
-                    gain[:, t : t + 1],
-                    inverses[half, t],
-                    ALU.mult,
-                    ALU.mult,
-                )
-            return z
+        def divide(z, t, start, inverse):
+            width = z.shape[-1]
+            nc.vector.scalar_tensor_tensor(
+                z, hidden[t][:, start : start + width], gain[:, t : t + 1], inverse, ALU.mult, ALU.mult
+            )
 
         def weave(copy, name, source, width):
             woven = sb(name, [P, width, PACK], BF16)
             copy(woven[:].rearrange("p (c i) t -> p c t i", i=4), source.rearrange("p t (c i) -> p c t i", i=4))
             return woven
 
-        def quantise_z(name, woven, width):
-            z_words = sb("z_words" + name, [P, width], U32)
+        def quantise_z(name, woven, z_words):
+            width = z_words.shape[-1]
             z_bytes = sb("z_bytes" + name, [P, width], U8)
             nc.vector.quantize_mx(z_words[:].bitcast(FP8X4), z_bytes[:], woven[:].rearrange("p n t -> p (n t)"))
             return z_words, z_bytes
 
-        def second_product(unit, second_words, z_words, z_bytes):
+        def second_product(unit, z_words, z_bytes):
             bank = psum.tile([P, PACK, UNIT], F32, name="product%d" % unit)
             for t in range(PACK):
                 cols = slice(P * t, P * (t + 1))
@@ -206,29 +201,69 @@ def tile_picked_pqdiv_none_po_kernel(
             nc.vector.quantize_mx(words[:].bitcast(FP8X4), out_bytes[:, cols], woven[:].rearrange("p n t -> p (n t)"))
             nc.sync.dma_start(out_words_dram[:, cols], words[:].bitcast(I32))
 
-        invert_pair(0, (0, 1), look_up(0, (0, 1), (None, None)))
-        invert_pair(0, (2, 3), look_up(0, (2, 3), (None, None)))
-        invert_pair(1, (0, 1), look_up(1, (0, 1), ("first0_2", "first0_3")))
-        z_low = divide(0)
-        total = look_up(1, (2, 3), ("inverse0_0", "inverse0_2"))
-        woven_low = weave(nc.scalar.copy, "z_woven0", z_low[:], HALF)
-        invert_apart(1, (2, 3), total)
-        second_words = deal_words("k2", second_picked, "z0")
-        z_words, z_bytes = quantise_z("0", woven_low, HALF)
+        low = []
+        for pair in range(2):
+            rows = (2 * pair, 2 * pair + 1)
+            low.append(
+                look_up(
+                    "_low%d" % pair,
+                    rows,
+                    0,
+                    [sb("first_low%d" % t, [P, HALF], F32) for t in rows],
+                    sb("total_low%d" % pair, [P, 2, HALF], F32, "sixteenth%d" % rows[1]),
+                    at(ROOTS + 2048, "root_low%d" % pair, [P, 2, HALF], F32),
+                )
+            )
+        high01 = look_up(
+            "_high01",
+            (0, 1),
+            HALF,
+            [sb("first_high%d" % t, [P, HALF], F32, "first_low%d" % (t + 2)) for t in (0, 1)],
+            sb("total_high01", [P, 2, HALF], F32),
+            at(ROOTS + 1024, "root_high01", [P, 2, HALF], F32),
+        )
+        z_low = sb("z_low", [P, PACK, HALF], BF16)
+        for t in range(PACK):
+            divide(z_low[:, t, :], t, 0, low[t // 2][:, t % 2, :])
+        woven_low = weave(nc.scalar.copy, "z_woven_low", z_low[:], HALF)
+        high23 = []
+        for n in range(2):
+            high23.append(
+                look_up(
+                    "_high23_%d" % n,
+                    (2, 3),
+                    HALF + UNIT * n,
+                    [at(ROOTS + 3072 + 512 * u, "first_high23_%d_%d" % (n, u), [P, UNIT], F32) for u in range(2)],
+                    at(TOTALS + 1536 + 2048 * n, "total_high23_%d" % n, [P, 2, UNIT], F32),
+                    sb("root_high23_%d" % n, [P, 2, UNIT], F32, "root_high23"),
+                )
+            )
+        z_words, z_bytes = quantise_z("_low", woven_low, at(TOTALS + 2048, "z_words_low", [P, HALF], U32))
         banks = []
         for unit in range(2):
             cols = slice(UNIT * unit, UNIT * (unit + 1))
-            banks.append(second_product(unit, second_words, z_words[:, cols], z_bytes[:, cols]))
-        z_high = divide(1, "z_woven0")
-        woven_high = []
-        for n in range(2):
-            woven_high.append(
-                weave(nc.vector.tensor_copy, "z_woven1_%d" % n, z_high[:, :, UNIT * n : UNIT * (n + 1)], UNIT)
-            )
-        for n in range(2):
-            z_words, z_bytes = quantise_z("1_%d" % n, woven_high[n], UNIT)
-            banks.append(second_product(2 + n, second_words, z_words[:], z_bytes[:]))
+            banks.append(second_product(unit, z_words[:, cols], z_bytes[:, cols]))
+        z_high = at(TOTALS, "z_high", [P, PACK, HALF], BF16)
 
+        def divide_high(n, rows):
+            cols = slice(UNIT * n, UNIT * (n + 1))
+            for t in rows:
+                inverse = high01[:, t, cols] if t < 2 else high23[n][:, t - 2, :]
+                divide(z_high[:, t, cols], t, HALF + UNIT * n, inverse)
+
+        def weave_high(n):
+            return weave(nc.vector.tensor_copy, "z_woven_high%d" % n, z_high[:, :, UNIT * n : UNIT * (n + 1)], UNIT)
+
+        def product_high(n, woven):
+            words, scale_bytes = quantise_z("_high%d" % n, woven, sb("z_words_high%d" % n, [P, UNIT], U32))
+            banks.append(second_product(2 + n, words[:], scale_bytes[:]))
+
+        divide_high(0, (0, 1, 2, 3))
+        divide_high(1, (0, 1))
+        woven = weave_high(0)
+        divide_high(1, (2, 3))
+        product_high(0, woven)
+        woven = weave_high(1)
         out_woven_low = sb("out_woven0", [P, HALF, PACK], BF16)
         for unit in range(2):
             nc.scalar.activation(
@@ -237,6 +272,7 @@ def tile_picked_pqdiv_none_po_kernel(
                 ACT.Copy,
                 scale=0.0625,
             )
+        product_high(1, woven)
         quantise_out("0", out_woven_low, slice(0, HALF), HALF)
         for unit in (2, 3):
             result = hand_out(unit, banks[unit])

@@ -116,7 +116,12 @@ def tile_picked_pqdiv_none_po_kernel(
                 .bitcast(I32)
                 .rearrange("p (c i t) -> p c t i", t=PACK, i=4),
             )
-        token_words = pick("token_words", x_word_table[:].bitcast(U32), U32, "offs")
+        token_words = sb("token_words", [P, S], U32)
+        for half in range(2):
+            nc.vector.tensor_copy(
+                token_words[:, HALF * half : HALF * (half + 1)],
+                x_word_table[:].bitcast(U32).indirect(lists["offs"][:, 16 * half : 16 * (half + 1)]),
+            )
         second_picked_words = at(0, "second_picked_words", [P, H], U32)
         nc.vector.tensor_copy(second_picked_words[:], d_word_table[:].bitcast(U32).indirect(lists["k2"][:]))
         second_bytes = at(4 * H, "second_bytes", [P, H], U8)
@@ -129,15 +134,17 @@ def tile_picked_pqdiv_none_po_kernel(
         for t in range(PACK):
             cols = slice(P * t, P * (t + 1))
             bank = psum.tile([P, S], F32, name="hidden%d" % t)
-            nc.tensor.matmul_mx(
-                bank[:],
-                lhsT=first_words[:, cols].bitcast(FP8X4),
-                lhsT_scale=first_bytes[:, cols],
-                rhs=token_words[:].bitcast(FP8X4),
-                rhs_scale=token_bytes[:],
-                start=True,
-                stop=True,
-            )
+            for half in range(2):
+                tokens = slice(HALF * half, HALF * (half + 1))
+                nc.tensor.matmul_mx(
+                    bank[:, tokens],
+                    lhsT=first_words[:, cols].bitcast(FP8X4),
+                    lhsT_scale=first_bytes[:, cols],
+                    rhs=token_words[:, tokens].bitcast(FP8X4),
+                    rhs_scale=token_bytes[:, tokens],
+                    start=True,
+                    stop=True,
+                )
             size = sb("size%d" % t, [P, S], F32)
             nc.scalar.activation(size[:], bank[:], ACT.Abs, bias=zero[:], scale=sixteenths[t][:])
             hidden.append(bank)
@@ -175,12 +182,11 @@ def tile_picked_pqdiv_none_po_kernel(
             nc.vector.quantize_mx(z_words[:].bitcast(FP8X4), z_bytes[:], woven[:].rearrange("p n t -> p (n t)"))
             return z_words, z_bytes
 
-        def second_product(unit, z_words, z_bytes):
-            bank = psum.tile([P, PACK, UNIT], F32, name="product%d" % unit)
-            for t in range(PACK):
+        def second_product(bank, rows, z_words, z_bytes):
+            for u, t in enumerate(rows):
                 cols = slice(P * t, P * (t + 1))
                 nc.tensor.matmul_mx(
-                    bank[:, t, :],
+                    bank[:, u, :],
                     lhsT=second_words[:, cols].bitcast(FP8X4),
                     lhsT_scale=second_bytes[:, cols],
                     rhs=z_words.bitcast(FP8X4),
@@ -190,10 +196,16 @@ def tile_picked_pqdiv_none_po_kernel(
                 )
             return bank
 
+        def whole_bank(unit):
+            return psum.tile([P, PACK, UNIT], F32, name="product%d" % unit)
+
+        def store(unit, result):
+            nc.sync.dma_start(out_rows[:, :, UNIT * unit : UNIT * (unit + 1)], result[:])
+
         def hand_out(unit, bank):
             result = sb("result%d" % unit, [P, PACK, UNIT], F32)
             nc.scalar.activation(result[:], bank[:], ACT.Copy, scale=0.0625)
-            nc.sync.dma_start(out_rows[:, :, UNIT * unit : UNIT * (unit + 1)], result[:])
+            store(unit, result)
             return result
 
         def quantise_out(name, woven, cols, width):
@@ -242,28 +254,31 @@ def tile_picked_pqdiv_none_po_kernel(
         banks = []
         for unit in range(2):
             cols = slice(UNIT * unit, UNIT * (unit + 1))
-            banks.append(second_product(unit, z_words[:, cols], z_bytes[:, cols]))
+            banks.append(second_product(whole_bank(unit), range(PACK), z_words[:, cols], z_bytes[:, cols]))
         z_high = at(TOTALS, "z_high", [P, PACK, HALF], BF16)
 
-        def divide_high(n, rows):
-            cols = slice(UNIT * n, UNIT * (n + 1))
-            for t in rows:
-                inverse = high01[:, t, cols] if t < 2 else high23[n][:, t - 2, :]
-                divide(z_high[:, t, cols], t, HALF + UNIT * n, inverse)
+        def divide_high23(n):
+            for t in (2, 3):
+                divide(z_high[:, t, UNIT * n : UNIT * (n + 1)], t, HALF + UNIT * n, high23[n][:, t - 2, :])
 
         def weave_high(n):
             return weave(nc.vector.tensor_copy, "z_woven_high%d" % n, z_high[:, :, UNIT * n : UNIT * (n + 1)], UNIT)
 
-        def product_high(n, woven):
-            words, scale_bytes = quantise_z("_high%d" % n, woven, sb("z_words_high%d" % n, [P, UNIT], U32))
-            banks.append(second_product(2 + n, words[:], scale_bytes[:]))
+        def quantise_high(n, woven):
+            return quantise_z("_high%d" % n, woven, sb("z_words_high%d" % n, [P, UNIT], U32))
 
-        divide_high(0, (0, 1, 2, 3))
-        divide_high(1, (0, 1))
-        woven = weave_high(0)
-        divide_high(1, (2, 3))
-        product_high(0, woven)
-        woven = weave_high(1)
+        divide(z_high[:, 0, :], 0, HALF, high01[:, 0, :])
+        divide_high23(0)
+        divide(z_high[:, 1, :], 1, HALF, high01[:, 1, :])
+        divide_high23(1)
+        woven = [weave_high(0), weave_high(1)]
+        z_words, z_bytes = quantise_high(0, woven[0])
+        banks.append(second_product(whole_bank(2), range(PACK), z_words[:], z_bytes[:]))
+        z_words, z_bytes = quantise_high(1, woven[1])
+        last_low = psum.tile([P, 2, UNIT], F32, name="product3")
+        last_high = psum.tile([P, 2, UNIT], F32, name="product3_high", tag="hidden0")
+        second_product(last_low, (0, 1), z_words[:], z_bytes[:])
+        second_product(last_high, (2, 3), z_words[:], z_bytes[:])
         out_woven_low = sb("out_woven0", [P, HALF, PACK], BF16)
         for unit in range(2):
             nc.scalar.activation(
@@ -272,15 +287,18 @@ def tile_picked_pqdiv_none_po_kernel(
                 ACT.Copy,
                 scale=0.0625,
             )
-        product_high(1, woven)
         quantise_out("0", out_woven_low, slice(0, HALF), HALF)
-        for unit in (2, 3):
-            result = hand_out(unit, banks[unit])
-            woven = weave(nc.vector.tensor_copy, "out_woven%d" % unit, result[:], UNIT)
-            quantise_out("%d" % unit, woven, slice(UNIT * unit, UNIT * (unit + 1)), UNIT)
+        result = hand_out(2, banks[2])
+        woven = weave(nc.vector.tensor_copy, "out_woven2", result[:], UNIT)
+        quantise_out("2", woven, slice(2 * UNIT, 3 * UNIT), UNIT)
+        result = sb("result3", [P, PACK, UNIT], F32)
+        nc.scalar.activation(result[:, 0:2, :], last_low[:], ACT.Copy, scale=0.0625)
+        nc.vector.tensor_scalar(result[:, 2:4, :], last_high[:], 0.0625, None, ALU.mult)
+        store(3, result)
+        woven = weave(nc.vector.tensor_copy, "out_woven3", result[:], UNIT)
+        quantise_out("3", woven, slice(3 * UNIT, 4 * UNIT), UNIT)
         for unit in (0, 1):
             hand_out(unit, banks[unit])
         out_scale_rows = out_2[0].bitcast(I32)
         for q in range(4):
-            queue = nc.sync if q % 2 == 0 else nc.scalar
-            queue.dma_start(out_scale_rows[4 * q : 4 * q + 4, :], out_bytes[32 * q : 32 * q + 4, :].bitcast(I32))
+            nc.sync.dma_start(out_scale_rows[4 * q : 4 * q + 4, :], out_bytes[32 * q : 32 * q + 4, :].bitcast(I32))

from contextlib import ExitStack

import concourse.mybir as mybir

F32 = mybir.dt.float32
BF16 = mybir.dt.bfloat16
I32 = mybir.dt.int32
U32 = mybir.dt.uint32
U16 = mybir.dt.uint16
U8 = mybir.dt.uint8
FP8X4 = mybir.dt.float8_e4m3fn_x4
ACT = mybir.ActivationFunctionType
ALU = mybir.AluOpType

P = 128
PACK = 4
K = 512
TABLE = 2048
S = 512
H = 512
LIST_COLS = 32
HALF = 256
UNIT = 128
ROOTS = 4 * TABLE
TOTALS = ROOTS + 4096

FLOPS = 2 * 2 * K * H * S


def tile_picked_pqdiv_none_po_kernel(
    tc, x_words, x_scales, d_words, d_scales, gs, offs, k1, n1, n2, k2, out_0, out_1, out_2
):
    nc = tc.nc
    with ExitStack() as ctx:
        pool = ctx.enter_context(tc.tile_pool(name="held", bufs=1))
        reused = ctx.enter_context(tc.tile_pool(name="reused", bufs=1))
        psum = ctx.enter_context(tc.psum_pool(name="psum", bufs=1))

        def sb(name, shape, dtype, tag=None):
            return pool.tile(shape, dtype, name=name, tag=tag or name, align_bytes=64)

        def at(offset, name, shape, dtype):
            return reused.tile(shape, dtype, name=name, align_bytes=64, offset=offset)

        lists = {name: sb("list_" + name, [P, LIST_COLS], U16) for name in ("offs", "k1", "n1", "n2", "k2")}
        d_word_table = sb("d_word_table", [P, TABLE], I32)
        x_word_table = at(0, "x_word_table", [P, TABLE], I32)
        d_byte_table = sb("d_byte_table", [P, TABLE], U8)
        x_byte_table = sb("x_byte_table", [P, TABLE], U8)
        gain = sb("gain", [P, PACK], F32)
        warm = sb("warm", [P, 2], F32)
        out_bytes = sb("out_bytes", [P, S], U8)

        token_bytes = sb("token_bytes", [P, S], U8)

        sixteenths = [sb("sixteenth%d" % t, [P, 1], F32) for t in range(PACK)]
        zero = at(ROOTS + 2048, "zero", [P, 1], F32)

        nc.vector.memset(x_byte_table[:].bitcast(I32), 0)
        nc.gpsimd.memset(d_byte_table[:].bitcast(I32), 0)
        nc.gpsimd.memset(warm[:, 0:1], 1.0)
        nc.gpsimd.memset(token_bytes[:].bitcast(I32), 0)
        nc.gpsimd.memset(zero[:], 0.0)
        for sixteenth in sixteenths:
            nc.gpsimd.memset(sixteenth[:], 0.0625)
        nc.scalar.activation(warm[:, 1:2], warm[:, 0:1], ACT.Abs_reciprocal_sqrt)

        nc.sync.dma_start(lists["k1"][:], k1)
        nc.sync.dma_start(lists["k2"][:], k2)
        nc.sync.dma_start(d_byte_table[0:P:8, :].bitcast(I32), d_scales[0].bitcast(I32))
        nc.sync.dma_start(lists["offs"][:], offs)
        nc.sync.dma_start(x_byte_table[0:P:8, :].bitcast(I32), x_scales[0].bitcast(I32))
        nc.sync.dma_start(d_word_table[:], d_words[0].rearrange("p n t -> p (n t)").bitcast(I32))
        nc.sync.dma_start(lists["n1"][:], n1)
        nc.sync.dma_start(lists["n2"][:], n2)
        nc.sync.dma_start(gain[:], gs.rearrange("(p t) o -> p (t o)", t=PACK))
        nc.sync.dma_start(x_word_table[:], x_words[0].rearrange("p n t -> p (n t)").bitcast(I32))

        def pick(name, table, dtype, index):
            picked = sb(name, [P, H], dtype)
            nc.vector.tensor_copy(picked[:], table.indirect(lists[index][:]))
            return picked

        def deal_bytes(dealt, picked):
            nc.vector.tensor_copy(
                dealt[:].rearrange("p (t c i) -> p c t i", t=PACK, i=16),
                picked[:].rearrange("p (c i t) -> p c t i", t=PACK, i=16),
            )
            for a in range(1, 4):
                nc.sync.dma_start(dealt[a:P:32, :].bitcast(I32), dealt[8 * a : P : 32, :].bitcast(I32))

        def deal_words(dealt, picked):
            nc.vector.tensor_copy(
                dealt[:].bitcast(I32).rearrange("p (t c i) -> p c t i", t=PACK, i=4),
                picked[:].bitcast(I32).rearrange("p (c i t) -> p c t i", t=PACK, i=4),
            )

        first_picked_bytes = pick("first_picked_bytes", d_byte_table[:], U8, "k1")
        second_picked_bytes = pick("second_picked_bytes", d_byte_table[:], U8, "k2")
        first_bytes = sb("first_bytes", [P, H], U8)
        deal_bytes(first_bytes, first_picked_bytes)
        token_picked_bytes = pick("token_picked_bytes", x_byte_table[:], U8, "offs")
        for a in range(4):
            nc.sync.dma_start(token_bytes[a:P:32, :].bitcast(I32), token_picked_bytes[8 * a : P : 32, :].bitcast(I32))
        first_picked_words = sb("first_picked_words", [P, H], U32)
        first_words = sb("first_words", [P, H], U32)
        for half in range(2):
            nc.vector.tensor_copy(
                first_picked_words[:, HALF * half : HALF * (half + 1)],
                d_word_table[:].bitcast(U32).indirect(lists["k1"][:, 16 * half : 16 * (half + 1)]),
            )
        for half in range(2):
            nc.vector.tensor_copy(
                first_words[:].bitcast(I32).rearrange("p (t c i) -> p c t i", t=PACK, i=4)[:, 16 * half : 16 * (half + 1)],
                first_picked_words[:, HALF * half : HALF * (half + 1)]
                .bitcast(I32)
                .rearrange("p (c i t) -> p c t i", t=PACK, i=4),
            )
        token_words = sb("token_words", [P, S], U32)
        for half in range(2):
            nc.vector.tensor_copy(
                token_words[:, HALF * half : HALF * (half + 1)],
                x_word_table[:].bitcast(U32).indirect(lists["offs"][:, 16 * half : 16 * (half + 1)]),
            )
        second_picked_words = at(0, "second_picked_words", [P, H], U32)
        nc.vector.tensor_copy(second_picked_words[:], d_word_table[:].bitcast(U32).indirect(lists["k2"][:]))
        second_bytes = at(4 * H, "second_bytes", [P, H], U8)
        deal_bytes(second_bytes, second_picked_bytes)
        second_words = sb("second_words", [P, H], U32)
        deal_words(second_words, second_picked_words)

        hidden = []
        sizes = []
        for t in range(PACK):
            cols = slice(P * t, P * (t + 1))
            bank = psum.tile([P, S], F32, name="hidden%d" % t)
            for half in range(2):
                tokens = slice(HALF * half, HALF * (half + 1))
                nc.tensor.matmul_mx(
                    bank[:, tokens],
                    lhsT=first_words[:, cols].bitcast(FP8X4),
                    lhsT_scale=first_bytes[:, cols],
                    rhs=token_words[:, tokens].bitcast(FP8X4),
                    rhs_scale=token_bytes[:, tokens],
                    start=True,
                    stop=True,
                )
            size = sb("size%d" % t, [P, S], F32)
            nc.scalar.activation(size[:], bank[:], ACT.Abs, bias=zero[:], scale=sixteenths[t][:])
            hidden.append(bank)
            sizes.append(size)

        out_rows = out_0.rearrange("(p t) j -> p t j", t=PACK)
        out_words_dram = out_1[0].rearrange("p n t -> p (n t)").bitcast(I32)

        def look_up(name, rows, start, firsts, total, root):
            width = total.shape[-1]
            entries = slice(start // 16, (start + width) // 16)
            for t, first in zip(rows, firsts):
                nc.vector.tensor_copy(first[:], sizes[t][:].indirect(lists["n1"][:, entries]))
            for u, t in enumerate(rows):
                nc.vector.tensor_tensor(total[:, u, :], sizes[t][:].indirect(lists["n2"][:, entries]), firsts[u][:], ALU.add)
            inverse = sb("inverse" + name, [P, 2, width], F32)
            nc.scalar.activation(root[:], total[:], ACT.Abs_reciprocal_sqrt, bias=0.5)
            nc.scalar.activation(inverse[:], root[:], ACT.Square, scale=0.25)
            return inverse

        def divide(z, t, start, inverse):
            width = z.shape[-1]
            nc.vector.scalar_tensor_tensor(
                z, hidden[t][:, start : start + width], gain[:, t : t + 1], inverse, ALU.mult, ALU.mult
            )

        def weave(copy, name, source, width):
            woven = sb(name, [P, width, PACK], BF16)
            copy(woven[:].rearrange("p (c i) t -> p c t i", i=4), source.rearrange("p t (c i) -> p c t i", i=4))
            return woven

        def quantise_z(name, woven, z_words):
            width = z_words.shape[-1]
            z_bytes = sb("z_bytes" + name, [P, width], U8)
            nc.vector.quantize_mx(z_words[:].bitcast(FP8X4), z_bytes[:], woven[:].rearrange("p n t -> p (n t)"))
            return z_words, z_bytes

        def second_product(bank, rows, z_words, z_bytes):
            for u, t in enumerate(rows):
                cols = slice(P * t, P * (t + 1))
                nc.tensor.matmul_mx(
                    bank[:, u, :],
                    lhsT=second_words[:, cols].bitcast(FP8X4),
                    lhsT_scale=second_bytes[:, cols],
                    rhs=z_words.bitcast(FP8X4),
                    rhs_scale=z_bytes,
                    start=True,
                    stop=True,
                )
            return bank

        def whole_bank(unit):
            return psum.tile([P, PACK, UNIT], F32, name="product%d" % unit)

        def store(unit, result):
            nc.sync.dma_start(out_rows[:, :, UNIT * unit : UNIT * (unit + 1)], result[:])

        def hand_out(unit, bank):
            result = sb("result%d" % unit, [P, PACK, UNIT], F32)
            nc.scalar.activation(result[:], bank[:], ACT.Copy, scale=0.0625)
            store(unit, result)
            return result

        def quantise_out(name, woven, cols, width):
            words = sb("out_words" + name, [P, width], U32)
            nc.vector.quantize_mx(words[:].bitcast(FP8X4), out_bytes[:, cols], woven[:].rearrange("p n t -> p (n t)"))
            nc.sync.dma_start(out_words_dram[:, cols], words[:].bitcast(I32))

        low = []
        for pair in range(2):
            rows = (2 * pair, 2 * pair + 1)
            low.append(
                look_up(
                    "_low%d" % pair,
                    rows,
                    0,
                    [sb("first_low%d" % t, [P, HALF], F32) for t in rows],
                    sb("total_low%d" % pair, [P, 2, HALF], F32, "sixteenth%d" % rows[1]),
                    at(ROOTS + 2048, "root_low%d" % pair, [P, 2, HALF], F32),
                )
            )
        high01 = look_up(
            "_high01",
            (0, 1),
            HALF,
            [sb("first_high%d" % t, [P, HALF], F32, "first_low%d" % (t + 2)) for t in (0, 1)],
            sb("total_high01", [P, 2, HALF], F32),
            at(ROOTS + 1024, "root_high01", [P, 2, HALF], F32),
        )
        z_low = sb("z_low", [P, PACK, HALF], BF16)
        for t in range(PACK):
            divide(z_low[:, t, :], t, 0, low[t // 2][:, t % 2, :])
        woven_low = weave(nc.scalar.copy, "z_woven_low", z_low[:], HALF)
        high23 = []
        for n in range(2):
            high23.append(
                look_up(
                    "_high23_%d" % n,
                    (2, 3),
                    HALF + UNIT * n,
                    [at(ROOTS + 3072 + 512 * u, "first_high23_%d_%d" % (n, u), [P, UNIT], F32) for u in range(2)],
                    at(TOTALS + 1536 + 2048 * n, "total_high23_%d" % n, [P, 2, UNIT], F32),
                    sb("root_high23_%d" % n, [P, 2, UNIT], F32, "root_high23"),
                )
            )
        z_words, z_bytes = quantise_z("_low", woven_low, at(TOTALS + 2048, "z_words_low", [P, HALF], U32))
        banks = []
        for unit in range(2):
            cols = slice(UNIT * unit, UNIT * (unit + 1))
            banks.append(second_product(whole_bank(unit), range(PACK), z_words[:, cols], z_bytes[:, cols]))
        z_high = at(TOTALS, "z_high", [P, PACK, HALF], BF16)

        def divide_high23(n):
            for t in (2, 3):
                divide(z_high[:, t, UNIT * n : UNIT * (n + 1)], t, HALF + UNIT * n, high23[n][:, t - 2, :])

        def weave_high(n):
            return weave(nc.vector.tensor_copy, "z_woven_high%d" % n, z_high[:, :, UNIT * n : UNIT * (n + 1)], UNIT)

        def quantise_high(n, woven):
            return quantise_z("_high%d" % n, woven, sb("z_words_high%d" % n, [P, UNIT], U32))

        divide(z_high[:, 0, :], 0, HALF, high01[:, 0, :])
        divide_high23(0)
        divide(z_high[:, 1, :], 1, HALF, high01[:, 1, :])
        divide_high23(1)
        woven = [weave_high(0), weave_high(1)]
        z_words, z_bytes = quantise_high(0, woven[0])
        banks.append(second_product(whole_bank(2), range(PACK), z_words[:], z_bytes[:]))
        z_words, z_bytes = quantise_high(1, woven[1])
        last_low = psum.tile([P, 2, UNIT], F32, name="product3")
        last_high = psum.tile([P, 2, UNIT], F32, name="product3_high", tag="hidden0")
        second_product(last_low, (0, 1), z_words[:], z_bytes[:])
        second_product(last_high, (2, 3), z_words[:], z_bytes[:])
        out_woven_low = sb("out_woven0", [P, HALF, PACK], BF16)
        for unit in range(2):
            nc.scalar.activation(
                out_woven_low[:, UNIT * unit : UNIT * (unit + 1), :],
                banks[unit][:].rearrange("p t n -> p n t"),
                ACT.Copy,
                scale=0.0625,
            )
        quantise_out("0", out_woven_low, slice(0, HALF), HALF)
        result = hand_out(2, banks[2])
        woven = weave(nc.vector.tensor_copy, "out_woven2", result[:], UNIT)
        quantise_out("2", woven, slice(2 * UNIT, 3 * UNIT), UNIT)
        result = sb("result3", [P, PACK, UNIT], F32)
        nc.scalar.activation(result[:, 0:2, :], last_low[:], ACT.Copy, scale=0.0625)
        nc.vector.tensor_scalar(result[:, 2:4, :], last_high[:], 0.0625, None, ALU.mult)
        store(3, result)
        woven = weave(nc.vector.tensor_copy, "out_woven3", result[:], UNIT)
        quantise_out("3", woven, slice(3 * UNIT, 4 * UNIT), UNIT)
        for unit in (0, 1):
            hand_out(unit, banks[unit])
        out_scale_rows = out_2[0].bitcast(I32)
        for q in range(4):
            nc.sync.dma_start(out_scale_rows[4 * q : 4 * q + 4, :], out_bytes[32 * q : 32 * q + 4, :].bitcast(I32))
